import numpy as np, ml_dtypes
CORES = [16,32,48,64,80]
N = 5
import mx_ref
NC = 512
BF = ml_dtypes.bfloat16
def setup_inputs(rng):
    def f(*shape):
        return mx_ref.flush((rng.standard_normal(shape, dtype=np.float32) * np.exp2(rng.integers(-2, 3, shape[:-1] + (1,)))).astype(BF))
    return {"w": f(N, 128, 512), "x": f(N, 128, 4 * NC)}
def setup_inputs_blocks(rng):
    d = setup_inputs(rng)
    for k in ("w", "x"): d[k] = mx_ref.spread(d[k], rng, 4)
    return d
def setup_inputs_wide(rng):
    d = setup_inputs(rng)
    for k in ("w", "x"): d[k] = mx_ref.flush((d[k].astype(np.float32) * np.exp2(rng.integers(-8, 9, (N, 1, 1))).astype(np.float32)).astype(BF))
    return d
def setup_inputs_zeros(rng):
    d = setup_inputs(rng); v = d["x"].reshape(N, 128, -1, 4).copy()
    v[np.broadcast_to((rng.random((N, 1, v.shape[2], 1)) < 0.33), v.shape)] = 0
    d["x"] = v.reshape(d["x"].shape)
    return d
def reference(w, x):
    QX = [mx_ref.quantize(x[j]) for j in range(N)]
    y = np.zeros((N, 128, NC), np.float32)
    for r in range(N):
        qw = mx_ref.quantize(w[r])
        for j in range(N):
            p = mx_ref.matmul(qw, QX[j])
            y[r] = p if j == 0 else np.maximum(y[r], p)
    return {"y": y}

@@ -1,0 +1,203 @@
+from concourse.bass import DstId, RemoteDMATransfer
+from concourse.mybir import dt, AluOpType
+
+N = 5
+NSIM = 96
+XW = 512
+WW = 128
+BANK = 512
+
+FULL = (("s", 0, XW), ("c", 0, XW))
+STRAIGHT = ()
+ACROSS = (("own", 1, 0),)
+FLOWS = (
+    (4, ACROSS, FULL),
+    (1, STRAIGHT, FULL),
+    (2, STRAIGHT, FULL),
+    (3, STRAIGHT, FULL),
+)
+LOADS = ((0, XW),)
+WHOLE = ((0, XW),)
+HALVES = ((0, XW // 2), (XW // 2, XW))
+PROC = ((0, WHOLE), (1, WHOLE), (2, WHOLE), (4, HALVES), (3, HALVES))
+
+
+def _arr(s, piece):
+    return "a%d%s%d" % (s, piece[0], piece[1])
+
+
+def _sem_names():
+    names = ["sent", "lw", "dw"]
+    names += ["lx%d" % i for i in range(len(LOADS))] + ["dx%d" % i for i in range(len(LOADS))]
+    for _, _, pieces in FLOWS:
+        for p in pieces:
+            names += [_arr(s, p) for s in range(N) if _arr(s, p) not in names]
+    for d, parts in PROC:
+        for k in range(len(parts)):
+            names += ["m%d_%d" % (d, k), "v%d_%d" % (d, k)]
+    names += ["st%d" % k for k in range(len(PROC[-1][1]))]
+    return names
+
+
+SCRATCH = {
+    "xb": ("sbuf", [128, 4 * XW], "bfloat16"),
+    "wb": ("sbuf", [128, 4 * WW], "bfloat16"),
+    "qw": ("sbuf", [128, WW], "float8_e4m3fn_x4"),
+    "sw": ("sbuf", [128, WW], "uint8"),
+    "acc": ("sbuf", [128, XW], "float32"),
+    "ps": ("psum", [128, BANK * sum(len(parts) for _, parts in PROC)], "float32"),
+}
+for _s in range(N):
+    SCRATCH["qx%d" % _s] = ("sbuf", [128, XW], "float8_e4m3fn_x4")
+    SCRATCH["sx%d" % _s] = ("sbuf", [128, XW], "uint8")
+SEMAPHORES = _sem_names()
+
+
+def _count(mask):
+    return bin(mask).count("1")
+
+
+def _width(piece):
+    return (piece[2] - piece[1]) * (4 if piece[0] == "c" else 1)
+
+
+def _view(T, s, piece):
+    kind, a, b = piece
+    if kind == "c":
+        return T["qx%d" % s][:, a:b].bitcast(dt.uint8)
+    return T["sx%d" % s][:, a:b]
+
+
+def _plan(T, topo):
+    cores = list(T.cores)
+    chips = sorted(set(topo.chip(c) for c in range(NSIM)))
+    out, got = {}, {}
+
+    def pick(chip, die, nxt, i):
+        return [c for c in range(NSIM) if topo.chip(c) == chip and topo.die(c) == die and c not in cores
+                and topo.may_write(c, nxt)][i]
+
+    for s, root in enumerate(cores):
+        away = topo.mask(root, cores[(s + 1) % N])
+        dies = sorted(set(topo.die(c) for c in range(NSIM)), key=lambda x: x != topo.die(root))
+        for d, way, pieces in FLOWS:
+            dst = cores[(s + d) % N]
+            path = [dst]
+            for where, other, i in reversed(way):
+                chip = topo.chip(root) if where == "own" else [c for c in chips if topo.mates(c, topo.chip(dst))][0]
+                path.insert(0, pick(chip, dies[other], path[0], i))
+            path.insert(0, root)
+            for piece in pieces:
+                for a, b in zip(path, path[1:]):
+                    if piece in got.setdefault((b, s), {}):
+                        continue
+                    mask = topo.mask(a, b)
+                    if a == root and topo.chip(a) == topo.chip(b):
+                        mask &= ~away
+                    out.setdefault(a, []).append((s, b, mask, piece))
+                    got[(b, s)][piece] = _count(mask)
+    return out, got
+
+
+def _send(g, T, topo, items):
+    if len(items) == 1:
+        s, child, mask, piece = items[0]
+        rid, pid, _ = topo.addr(child)
+        g.remote_dma(_view(T, s, piece), _view(T, s, piece), T.sem[_arr(s, piece)], T.sem.sent, pid, rid, mask)
+    else:
+        trs = []
+        for s, child, mask, piece in items:
+            rid, pid, _ = topo.addr(child)
+            trs.append(RemoteDMATransfer(dst_ids=[DstId(rid=rid, pnc=pid)], dma_engine_mask=mask,
+                                         remote_sem=T.sem[_arr(s, piece)], src=_view(T, s, piece),
+                                         dst=_view(T, s, piece)))
+        g.remote_dma_fused(trs, local_sem=T.sem.sent)
+    return sum(_count(it[2]) for it in items)
+
+
+def rank_program(g, core, T, topo):
+    rank = T.rank_of(core)
+    out, got = _plan(T, topo)
+    sends = out.get(core, [])
+    if rank is None and not sends:
+        return
+    sent = 0
+
+    if rank is None:
+        for s, child, mask, piece in sends:
+            g.wait_ge(T.sem[_arr(s, piece)], got[(core, s)][piece])
+            sent += _send(g, T, topo, [(s, child, mask, piece)])
+        g.wait_ge(T.sem.sent, sent)
+        return
+
+    qx, sx = T["qx%d" % rank], T["sx%d" % rank]
+
+    for i, (a, b) in enumerate(LOADS):
+        g.sync.dma_start(T.xb[:, 4 * a:4 * b], T.x[:, 4 * a:4 * b]).then_inc(T.sem["lx%d" % i], 16)
+    g.sync.dma_start(T.wb[:], T.w[:]).then_inc(T.sem.lw, 16)
+    for i, (a, b) in enumerate(LOADS):
+        g.vector.wait_ge(T.sem["lx%d" % i], 16)
+        g.vector.quantize_mx(qx[:, a:b], sx[:, a:b], T.xb[:, 4 * a:4 * b]).then_inc(T.sem["dx%d" % i], 1)
+    g.vector.wait_ge(T.sem.lw, 16)
+    g.vector.quantize_mx(T.qw[:], T.sw[:], T.wb[:]).then_inc(T.sem.dw, 1)
+
+    near = [it for it in sends if topo.chip(it[1]) == topo.chip(core)]
+    far = [it for it in sends if topo.chip(it[1]) != topo.chip(core)]
+    ready = set()
+
+    def need(piece):
+        for i, (a, b) in enumerate(LOADS):
+            if a < piece[2] and piece[1] < b and i not in ready:
+                ready.add(i)
+                g.wait_ge(T.sem["dx%d" % i], 1)
+
+    for k in range(max(len(near), len(far))):
+        pair = [lst[k] for lst in (near, far) if k < len(lst)]
+        for it in pair:
+            need(it[3])
+        if len(pair) == 2 and _width(pair[0][3]) != _width(pair[1][3]):
+            sent += _send(g, T, topo, pair[:1]) + _send(g, T, topo, pair[1:])
+        else:
+            sent += _send(g, T, topo, pair)
+    g.wait_ge(T.sem.sent, sent)
+
+    g.tensor.wait_ge(T.sem.dw, 1)
+    bank = 0
+    banks = {}
+    for d, parts in PROC:
+        s = (rank - d) % N
+        for k, (a, b) in enumerate(parts):
+            if d == 0:
+                for i, (la, lb) in enumerate(LOADS):
+                    if la < b and a < lb:
+                        g.tensor.wait_ge(T.sem["dx%d" % i], 1)
+            else:
+                for piece, n in got[(core, s)].items():
+                    if piece[1] < b and a < piece[2]:
+                        g.tensor.wait_ge(T.sem[_arr(s, piece)], n)
+            banks[(d, k)] = T.ps[:, BANK * bank:BANK * bank + (b - a)]
+            g.tensor.matmul_mx(banks[(d, k)], T.qw[:], T.sw[:], T["qx%d" % s][:, a:b], T["sx%d" % s][:, a:b],
+                               True, True).then_inc(T.sem["m%d_%d" % (d, k)], 1)
+            bank += 1
+
+    prev = None
+    for d, parts in PROC:
+        for k, (a, b) in enumerate(parts):
+            g.vector.wait_ge(T.sem["m%d_%d" % (d, k)], 1)
+            if prev is None:
+                op = g.vector.tensor_copy(T.acc[:, a:b], banks[(d, k)])
+            else:
+                for j, (pa, pb) in enumerate(prev[1]):
+                    if pa < b and a < pb:
+                        g.vector.wait_ge(T.sem["v%d_%d" % (prev[0], j)], 1)
+                op = g.vector.tensor_tensor(T.acc[:, a:b], banks[(d, k)], T.acc[:, a:b], AluOpType.max)
+            op.then_inc(T.sem["v%d_%d" % (d, k)], 1)
+        prev = (d, parts)
+
+    queues = (g.sync, g.scalar)
+    for k, (a, b) in enumerate(prev[1]):
+        q = queues[k % 2]
+        q.wait_ge(T.sem["v%d_%d" % (prev[0], k)], 1)
+        q.dma_start(T.y[:, a:b], T.acc[:, a:b]).then_inc(T.sem["st%d" % k], 16)
+    for k in range(len(prev[1])):
+        queues[k % 2].wait_ge(T.sem["st%d" % k], 16)

@@ -8,15 +8,16 @@ WW = 128
 BANK = 512
 
 FULL = (("s", 0, XW), ("c", 0, XW))
+EARLY = (("c", 0, WW), ("s", 0, XW), ("c", WW, XW))
 STRAIGHT = ()
 ACROSS = (("own", 1, 0),)
 FLOWS = (
-    (4, ACROSS, FULL),
-    (1, STRAIGHT, FULL),
+    (4, ACROSS, EARLY),
+    (1, STRAIGHT, EARLY),
     (2, STRAIGHT, FULL),
     (3, STRAIGHT, FULL),
 )
-LOADS = ((0, XW),)
+LOADS = ((0, WW), (WW, XW))
 WHOLE = ((0, XW),)
 HALVES = ((0, XW // 2), (XW // 2, XW))
 PROC = ((0, WHOLE), (1, WHOLE), (2, WHOLE), (4, HALVES), (3, HALVES))

@@ -7,20 +7,18 @@ XW = 512
 WW = 128
 BANK = 512
 
-FULL = (("s", 0, XW), ("c", 0, XW))
-EARLY = (("c", 0, WW), ("s", 0, XW), ("c", WW, XW))
+S, C = ("s", 0, XW), ("c", 0, XW)
+CA, CB = ("c", 0, 128), ("c", 128, XW)
 STRAIGHT = ()
-ACROSS = (("own", 1, 0),)
+H1 = (("own", 1, 0),)
 FLOWS = (
-    (4, ACROSS, EARLY),
-    (1, STRAIGHT, EARLY),
-    (2, STRAIGHT, FULL),
-    (3, STRAIGHT, FULL),
+    (4, H1, (CA, S)), (3, H1, (S,)), (4, H1, (CB,)),
+    (1, STRAIGHT, (CA, S, CB)),
+    (2, STRAIGHT, (S, C)),
+    (3, STRAIGHT, (C,)),
 )
-LOADS = ((0, WW), (WW, XW))
-WHOLE = ((0, XW),)
-HALVES = ((0, XW // 2), (XW // 2, XW))
-PROC = ((0, WHOLE), (1, WHOLE), (2, WHOLE), (4, HALVES), (3, HALVES))
+LOADS = ((0, 128), (128, XW))
+STEPS = ((0, 0, XW), (1, 0, XW), (2, 0, XW), (4, 0, 256), (4, 256, XW), (3, 0, 256), (3, 256, XW))
 
 
 def _arr(s, piece):
@@ -33,10 +31,8 @@ def _sem_names():
     for _, _, pieces in FLOWS:
         for p in pieces:
             names += [_arr(s, p) for s in range(N) if _arr(s, p) not in names]
-    for d, parts in PROC:
-        for k in range(len(parts)):
-            names += ["m%d_%d" % (d, k), "v%d_%d" % (d, k)]
-    names += ["st%d" % k for k in range(len(PROC[-1][1]))]
+    for k in range(len(STEPS)):
+        names += ["m%d" % k, "v%d" % k, "st%d" % k]
     return names
 
 
@@ -46,7 +42,7 @@ SCRATCH = {
     "qw": ("sbuf", [128, WW], "float8_e4m3fn_x4"),
     "sw": ("sbuf", [128, WW], "uint8"),
     "acc": ("sbuf", [128, XW], "float32"),
-    "ps": ("psum", [128, BANK * sum(len(parts) for _, parts in PROC)], "float32"),
+    "ps": ("psum", [128, BANK * len(STEPS)], "float32"),
 }
 for _s in range(N):
     SCRATCH["qx%d" % _s] = ("sbuf", [128, XW], "float8_e4m3fn_x4")
@@ -163,42 +159,41 @@ def rank_program(g, core, T, topo):
     g.wait_ge(T.sem.sent, sent)
 
     g.tensor.wait_ge(T.sem.dw, 1)
-    bank = 0
-    banks = {}
-    for d, parts in PROC:
+    banks = []
+    for k, (d, a, b) in enumerate(STEPS):
         s = (rank - d) % N
-        for k, (a, b) in enumerate(parts):
-            if d == 0:
-                for i, (la, lb) in enumerate(LOADS):
-                    if la < b and a < lb:
-                        g.tensor.wait_ge(T.sem["dx%d" % i], 1)
-            else:
-                for piece, n in got[(core, s)].items():
-                    if piece[1] < b and a < piece[2]:
-                        g.tensor.wait_ge(T.sem[_arr(s, piece)], n)
-            banks[(d, k)] = T.ps[:, BANK * bank:BANK * bank + (b - a)]
-            g.tensor.matmul_mx(banks[(d, k)], T.qw[:], T.sw[:], T["qx%d" % s][:, a:b], T["sx%d" % s][:, a:b],
-                               True, True).then_inc(T.sem["m%d_%d" % (d, k)], 1)
-            bank += 1
+        if d == 0:
+            for i, (la, lb) in enumerate(LOADS):
+                if la < b and a < lb:
+                    g.tensor.wait_ge(T.sem["dx%d" % i], 1)
+        else:
+            for piece, n in got[(core, s)].items():
+                if piece[1] < b and a < piece[2]:
+                    g.tensor.wait_ge(T.sem[_arr(s, piece)], n)
+        banks.append(T.ps[:, BANK * k:BANK * k + (b - a)])
+        g.tensor.matmul_mx(banks[k], T.qw[:], T.sw[:], T["qx%d" % s][:, a:b], T["sx%d" % s][:, a:b],
+                           True, True).then_inc(T.sem["m%d" % k], 1)
 
-    prev = None
-    for d, parts in PROC:
-        for k, (a, b) in enumerate(parts):
-            g.vector.wait_ge(T.sem["m%d_%d" % (d, k)], 1)
-            if prev is None:
-                op = g.vector.tensor_copy(T.acc[:, a:b], banks[(d, k)])
-            else:
-                for j, (pa, pb) in enumerate(prev[1]):
-                    if pa < b and a < pb:
-                        g.vector.wait_ge(T.sem["v%d_%d" % (prev[0], j)], 1)
-                op = g.vector.tensor_tensor(T.acc[:, a:b], banks[(d, k)], T.acc[:, a:b], AluOpType.max)
-            op.then_inc(T.sem["v%d_%d" % (d, k)], 1)
-        prev = (d, parts)
+    last = {}
+    for k, (d, a, b) in enumerate(STEPS):
+        g.vector.wait_ge(T.sem["m%d" % k], 1)
+        before = sorted(set(last[c] for c in range(a, b) if c in last))
+        for j in before:
+            g.vector.wait_ge(T.sem["v%d" % j], 1)
+        if before:
+            op = g.vector.tensor_tensor(T.acc[:, a:b], banks[k], T.acc[:, a:b], AluOpType.max)
+        else:
+            op = g.vector.tensor_copy(T.acc[:, a:b], banks[k])
+        op.then_inc(T.sem["v%d" % k], 1)
+        for c in range(a, b):
+            last[c] = k
 
     queues = (g.sync, g.scalar)
-    for k, (a, b) in enumerate(prev[1]):
-        q = queues[k % 2]
-        q.wait_ge(T.sem["v%d_%d" % (prev[0], k)], 1)
-        q.dma_start(T.y[:, a:b], T.acc[:, a:b]).then_inc(T.sem["st%d" % k], 16)
-    for k in range(len(prev[1])):
-        queues[k % 2].wait_ge(T.sem["st%d" % k], 16)
+    final = sorted(set(last.values()))
+    for i, k in enumerate(final):
+        cols = [c for c in last if last[c] == k]
+        a, b = min(cols), max(cols) + 1
+        queues[i % 2].wait_ge(T.sem["v%d" % k], 1)
+        queues[i % 2].dma_start(T.y[:, a:b], T.acc[:, a:b]).then_inc(T.sem["st%d" % k], 16)
+    for i, k in enumerate(final):
+        queues[i % 2].wait_ge(T.sem["st%d" % k], 16)

@@ -8,14 +8,16 @@ WW = 128
 BANK = 512
 
 S, C = ("s", 0, XW), ("c", 0, XW)
-CA, CB = ("c", 0, 128), ("c", 128, XW)
+CA, CBC = ("c", 0, 128), ("c", 128, XW)
 STRAIGHT = ()
 H1 = (("own", 1, 0),)
+H2 = (("own", 1, 1),)
 FLOWS = (
-    (4, H1, (CA, S)), (3, H1, (S,)), (4, H1, (CB,)),
-    (1, STRAIGHT, (CA, S, CB)),
-    (2, STRAIGHT, (S, C)),
-    (3, STRAIGHT, (C,)),
+    (4, H1, (CA,), 0), (1, STRAIGHT, (CA,), 0),
+    (2, H2, (S,), 1), (4, H2, (S,), 1), (3, H2, (S,), 1), (1, STRAIGHT, (S,), 1),
+    (4, H1, (CBC,), 2), (1, STRAIGHT, (CBC,), 2),
+    (2, STRAIGHT, (C,), 3),
+    (3, STRAIGHT, (C,), 4),
 )
 LOADS = ((0, 128), (128, XW))
 STEPS = ((0, 0, XW), (1, 0, XW), (2, 0, XW), (4, 0, 256), (4, 256, XW), (3, 0, 256), (3, 256, XW))
@@ -28,7 +30,7 @@ def _arr(s, piece):
 def _sem_names():
     names = ["sent", "lw", "dw"]
     names += ["lx%d" % i for i in range(len(LOADS))] + ["dx%d" % i for i in range(len(LOADS))]
-    for _, _, pieces in FLOWS:
+    for _, _, pieces, _ in FLOWS:
         for p in pieces:
             names += [_arr(s, p) for s in range(N) if _arr(s, p) not in names]
     for k in range(len(STEPS)):
@@ -54,10 +56,6 @@ def _count(mask):
     return bin(mask).count("1")
 
 
-def _width(piece):
-    return (piece[2] - piece[1]) * (4 if piece[0] == "c" else 1)
-
-
 def _view(T, s, piece):
     kind, a, b = piece
     if kind == "c":
@@ -77,7 +75,7 @@ def _plan(T, topo):
     for s, root in enumerate(cores):
         away = topo.mask(root, cores[(s + 1) % N])
         dies = sorted(set(topo.die(c) for c in range(NSIM)), key=lambda x: x != topo.die(root))
-        for d, way, pieces in FLOWS:
+        for d, way, pieces, call in FLOWS:
             dst = cores[(s + d) % N]
             path = [dst]
             for where, other, i in reversed(way):
@@ -91,7 +89,7 @@ def _plan(T, topo):
                     mask = topo.mask(a, b)
                     if a == root and topo.chip(a) == topo.chip(b):
                         mask &= ~away
-                    out.setdefault(a, []).append((s, b, mask, piece))
+                    out.setdefault(a, []).append((s, b, mask, piece, call))
                     got[(b, s)][piece] = _count(mask)
     return out, got
 
@@ -121,7 +119,7 @@ def rank_program(g, core, T, topo):
     sent = 0
 
     if rank is None:
-        for s, child, mask, piece in sends:
+        for s, child, mask, piece, _ in sends:
             g.wait_ge(T.sem[_arr(s, piece)], got[(core, s)][piece])
             sent += _send(g, T, topo, [(s, child, mask, piece)])
         g.wait_ge(T.sem.sent, sent)
@@ -138,24 +136,14 @@ def rank_program(g, core, T, topo):
     g.vector.wait_ge(T.sem.lw, 16)
     g.vector.quantize_mx(T.qw[:], T.sw[:], T.wb[:]).then_inc(T.sem.dw, 1)
 
-    near = [it for it in sends if topo.chip(it[1]) == topo.chip(core)]
-    far = [it for it in sends if topo.chip(it[1]) != topo.chip(core)]
     ready = set()
-
-    def need(piece):
+    for call in sorted(set(it[4] for it in sends)):
+        items = [it[:4] for it in sends if it[4] == call]
         for i, (a, b) in enumerate(LOADS):
-            if a < piece[2] and piece[1] < b and i not in ready:
+            if i not in ready and any(a < it[3][2] and it[3][1] < b for it in items):
                 ready.add(i)
                 g.wait_ge(T.sem["dx%d" % i], 1)
-
-    for k in range(max(len(near), len(far))):
-        pair = [lst[k] for lst in (near, far) if k < len(lst)]
-        for it in pair:
-            need(it[3])
-        if len(pair) == 2 and _width(pair[0][3]) != _width(pair[1][3]):
-            sent += _send(g, T, topo, pair[:1]) + _send(g, T, topo, pair[1:])
-        else:
-            sent += _send(g, T, topo, pair)
+        sent += _send(g, T, topo, items)
     g.wait_ge(T.sem.sent, sent)
 
     g.tensor.wait_ge(T.sem.dw, 1)

from concourse.bass import DstId, RemoteDMATransfer
from concourse.mybir import dt, AluOpType

N = 5
NSIM = 96
XW = 512
WW = 128
BANK = 512

S, C = ("s", 0, XW), ("c", 0, XW)
CA, CBC = ("c", 0, 128), ("c", 128, XW)
STRAIGHT = ()
H1 = (("own", 1, 0),)
H2 = (("own", 1, 1),)
FLOWS = (
    (4, H1, (CA,), 0), (1, STRAIGHT, (CA,), 0),
    (2, H2, (S,), 1), (4, H2, (S,), 1), (3, H2, (S,), 1), (1, STRAIGHT, (S,), 1),
    (4, H1, (CBC,), 2), (1, STRAIGHT, (CBC,), 2),
    (2, STRAIGHT, (C,), 3),
    (3, STRAIGHT, (C,), 4),
)
LOADS = ((0, 128), (128, XW))
STEPS = ((0, 0, XW), (1, 0, XW), (2, 0, XW), (4, 0, 256), (4, 256, XW), (3, 0, 256), (3, 256, XW))


def _arr(s, piece):
    return "a%d%s%d" % (s, piece[0], piece[1])


def _sem_names():
    names = ["sent", "lw", "dw"]
    names += ["lx%d" % i for i in range(len(LOADS))] + ["dx%d" % i for i in range(len(LOADS))]
    for _, _, pieces, _ in FLOWS:
        for p in pieces:
            names += [_arr(s, p) for s in range(N) if _arr(s, p) not in names]
    for k in range(len(STEPS)):
        names += ["m%d" % k, "v%d" % k, "st%d" % k]
    return names


SCRATCH = {
    "xb": ("sbuf", [128, 4 * XW], "bfloat16"),
    "wb": ("sbuf", [128, 4 * WW], "bfloat16"),
    "qw": ("sbuf", [128, WW], "float8_e4m3fn_x4"),
    "sw": ("sbuf", [128, WW], "uint8"),
    "acc": ("sbuf", [128, XW], "float32"),
    "ps": ("psum", [128, BANK * len(STEPS)], "float32"),
}
for _s in range(N):
    SCRATCH["qx%d" % _s] = ("sbuf", [128, XW], "float8_e4m3fn_x4")
    SCRATCH["sx%d" % _s] = ("sbuf", [128, XW], "uint8")
SEMAPHORES = _sem_names()


def _count(mask):
    return bin(mask).count("1")


def _view(T, s, piece):
    kind, a, b = piece
    if kind == "c":
        return T["qx%d" % s][:, a:b].bitcast(dt.uint8)
    return T["sx%d" % s][:, a:b]


def _plan(T, topo):
    cores = list(T.cores)
    chips = sorted(set(topo.chip(c) for c in range(NSIM)))
    out, got = {}, {}

    def pick(chip, die, nxt, i):
        return [c for c in range(NSIM) if topo.chip(c) == chip and topo.die(c) == die and c not in cores
                and topo.may_write(c, nxt)][i]

    for s, root in enumerate(cores):
        away = topo.mask(root, cores[(s + 1) % N])
        dies = sorted(set(topo.die(c) for c in range(NSIM)), key=lambda x: x != topo.die(root))
        for d, way, pieces, call in FLOWS:
            dst = cores[(s + d) % N]
            path = [dst]
            for where, other, i in reversed(way):
                chip = topo.chip(root) if where == "own" else [c for c in chips if topo.mates(c, topo.chip(dst))][0]
                path.insert(0, pick(chip, dies[other], path[0], i))
            path.insert(0, root)
            for piece in pieces:
                for a, b in zip(path, path[1:]):
                    if piece in got.setdefault((b, s), {}):
                        continue
                    mask = topo.mask(a, b)
                    if a == root and topo.chip(a) == topo.chip(b):
                        mask &= ~away
                    out.setdefault(a, []).append((s, b, mask, piece, call))
                    got[(b, s)][piece] = _count(mask)
    return out, got


def _send(g, T, topo, items):
    if len(items) == 1:
        s, child, mask, piece = items[0]
        rid, pid, _ = topo.addr(child)
        g.remote_dma(_view(T, s, piece), _view(T, s, piece), T.sem[_arr(s, piece)], T.sem.sent, pid, rid, mask)
    else:
        trs = []
        for s, child, mask, piece in items:
            rid, pid, _ = topo.addr(child)
            trs.append(RemoteDMATransfer(dst_ids=[DstId(rid=rid, pnc=pid)], dma_engine_mask=mask,
                                         remote_sem=T.sem[_arr(s, piece)], src=_view(T, s, piece),
                                         dst=_view(T, s, piece)))
        g.remote_dma_fused(trs, local_sem=T.sem.sent)
    return sum(_count(it[2]) for it in items)


def rank_program(g, core, T, topo):
    rank = T.rank_of(core)
    out, got = _plan(T, topo)
    sends = out.get(core, [])
    if rank is None and not sends:
        return
    sent = 0

    if rank is None:
        for s, child, mask, piece, _ in sends:
            g.wait_ge(T.sem[_arr(s, piece)], got[(core, s)][piece])
            sent += _send(g, T, topo, [(s, child, mask, piece)])
        g.wait_ge(T.sem.sent, sent)
        return

    qx, sx = T["qx%d" % rank], T["sx%d" % rank]

    for i, (a, b) in enumerate(LOADS):
        g.sync.dma_start(T.xb[:, 4 * a:4 * b], T.x[:, 4 * a:4 * b]).then_inc(T.sem["lx%d" % i], 16)
    g.sync.dma_start(T.wb[:], T.w[:]).then_inc(T.sem.lw, 16)
    for i, (a, b) in enumerate(LOADS):
        g.vector.wait_ge(T.sem["lx%d" % i], 16)
        g.vector.quantize_mx(qx[:, a:b], sx[:, a:b], T.xb[:, 4 * a:4 * b]).then_inc(T.sem["dx%d" % i], 1)
    g.vector.wait_ge(T.sem.lw, 16)
    g.vector.quantize_mx(T.qw[:], T.sw[:], T.wb[:]).then_inc(T.sem.dw, 1)

    ready = set()
    for call in sorted(set(it[4] for it in sends)):
        items = [it[:4] for it in sends if it[4] == call]
        for i, (a, b) in enumerate(LOADS):
            if i not in ready and any(a < it[3][2] and it[3][1] < b for it in items):
                ready.add(i)
                g.wait_ge(T.sem["dx%d" % i], 1)
        sent += _send(g, T, topo, items)
    g.wait_ge(T.sem.sent, sent)

    g.tensor.wait_ge(T.sem.dw, 1)
    banks = []
    for k, (d, a, b) in enumerate(STEPS):
        s = (rank - d) % N
        if d == 0:
            for i, (la, lb) in enumerate(LOADS):
                if la < b and a < lb:
                    g.tensor.wait_ge(T.sem["dx%d" % i], 1)
        else:
            for piece, n in got[(core, s)].items():
                if piece[1] < b and a < piece[2]:
                    g.tensor.wait_ge(T.sem[_arr(s, piece)], n)
        banks.append(T.ps[:, BANK * k:BANK * k + (b - a)])
        g.tensor.matmul_mx(banks[k], T.qw[:], T.sw[:], T["qx%d" % s][:, a:b], T["sx%d" % s][:, a:b],
                           True, True).then_inc(T.sem["m%d" % k], 1)

    last = {}
    for k, (d, a, b) in enumerate(STEPS):
        g.vector.wait_ge(T.sem["m%d" % k], 1)
        before = sorted(set(last[c] for c in range(a, b) if c in last))
        for j in before:
            g.vector.wait_ge(T.sem["v%d" % j], 1)
        if before:
            op = g.vector.tensor_tensor(T.acc[:, a:b], banks[k], T.acc[:, a:b], AluOpType.max)
        else:
            op = g.vector.tensor_copy(T.acc[:, a:b], banks[k])
        op.then_inc(T.sem["v%d" % k], 1)
        for c in range(a, b):
            last[c] = k

    queues = (g.sync, g.scalar)
    final = sorted(set(last.values()))
    for i, k in enumerate(final):
        cols = [c for c in last if last[c] == k]
        a, b = min(cols), max(cols) + 1
        queues[i % 2].wait_ge(T.sem["v%d" % k], 1)
        queues[i % 2].dma_start(T.y[:, a:b], T.acc[:, a:b]).then_inc(T.sem["st%d" % k], 16)
    for i, k in enumerate(final):
        queues[i % 2].wait_ge(T.sem["st%d" % k], 16)
